import numpy as np
import ml_dtypes


def mxq(x, axis, fmt="e4m3"):
    dtype, down = {"e4m3": (ml_dtypes.float8_e4m3fn, 7), "e5m2": (ml_dtypes.float8_e5m2, 14)}[fmt]
    v = np.moveaxis(np.asarray(x, np.float32).astype(ml_dtypes.bfloat16).astype(np.float64), axis, -1)
    blocks = v.reshape(v.shape[:-1] + (-1, 32))
    amax = np.abs(blocks).max(-1, keepdims=True)
    byte = np.maximum(np.where(amax > 0, np.frexp(amax)[1] - 1 + 127, 0) - down, 1)
    scale = np.exp2(byte - 127.0)
    codes = (blocks / scale).astype(np.float32).astype(dtype).astype(np.float64)
    return np.moveaxis((codes * scale).reshape(v.shape), -1, axis)


WIDE = False


def mx_kscale(k):
    if not WIDE:
        return np.ones(k)
    levels = np.array([30, -30])
    if k % 512:
        return np.exp2(np.random.permutation(np.resize(levels, k // 32))).repeat(32)
    a = np.empty((k // 512, 16))
    for p in range(k // 512):
        a[p, :8] = np.random.permutation(np.resize(levels, 8))
        for g in range(8):
            far = levels[np.abs(levels - a[p, g]) >= 10]
            a[p, g + 8] = far[np.random.randint(len(far))]
    return np.exp2(a.ravel()).repeat(32)


def f64(x):
    return np.asarray(x).astype(np.float64)


E2M1 = np.array([0.0, 0.5, 1.0, 1.5, 2.0, 3.0, 4.0, 6.0, -0.0, -0.5, -1.0, -1.5, -2.0, -3.0, -4.0, -6.0])


def pack_weight(w, fmt):
    k, n = w.shape
    w = f64(np.asarray(w, np.float32).astype(ml_dtypes.bfloat16)).reshape(k // 32, 32, n)
    amax = np.abs(w).max(1)
    if fmt == "e4m3":
        byte = np.frexp(amax)[1] - 1 + 127 - 7
    else:
        mant, ex = np.frexp(amax / 6.0)
        byte = np.where(mant > 0.5, ex, ex - 1) + 127
    byte = np.clip(np.where(amax > 0, byte, 1), 1, 254)
    scaled = (w * np.exp2(127.0 - byte)[:, None, :]).reshape(k, n).astype(np.float32)
    by_word = np.ascontiguousarray(scaled.reshape(k // 512, 128, 4, n).transpose(0, 1, 3, 2))
    if fmt == "e4m3":
        words = by_word.astype(ml_dtypes.float8_e4m3fn).view(np.uint8)
    else:
        c = by_word.astype(ml_dtypes.float4_e2m1fn).view(np.uint8) & 0xF
        words = (c[..., 0::2] | (c[..., 1::2] << 4)).reshape(k // 512, 128, 2 * n)
    return np.ascontiguousarray(words), np.ascontiguousarray(byte.astype(np.uint8).reshape(k // 512, 16, n))


def unpack_weight(words, scales, fmt):
    g, _, n = scales.shape
    words = np.ascontiguousarray(words).reshape(g, 128, n, -1)
    if fmt == "e4m3":
        vals = words.view(ml_dtypes.float8_e4m3fn).astype(np.float64)
    else:
        nib = np.empty((g, 128, n, 4), np.uint8)
        nib[..., 0::2] = words & 0xF
        nib[..., 1::2] = words >> 4
        vals = E2M1[nib]
    vals = vals * np.repeat(np.exp2(scales.astype(np.float64) - 127.0), 8, axis=1)[..., None]
    return vals.transpose(0, 1, 3, 2).reshape(g * 512, n)


def gelu(v):
    return 0.5 * v * (1.0 + np.tanh(np.sqrt(2.0 / np.pi) * (v + 0.044715 * v**3)))


K, L, R, M, T = 512, 512, 1024, 1024, 1024


def setup_inputs():
    n = np.random.standard_normal
    s1 = mx_kscale(K)[:, None]
    s2 = mx_kscale(L)[:, None]
    u = mx_kscale(R)[:, None]
    p_w = pack_weight(n((R, M)) / np.sqrt(R) / u, "e2m1")
    return {
        "x": (n((K, T)) * s1).astype(np.float32),
        "wx": (n((K, R)) / np.sqrt(K) / s1 * u.T).astype(np.float32),
        "c": (n((L, T)) * s2).astype(np.float32),
        "wc": (n((L, R)) / np.sqrt(L) / s2).astype(np.float32),
        "w_words": p_w[0],
        "w_scales": p_w[1],
        "b": (0.3 * n(1024)).astype(np.float32),
    }


def reference(x, wx, c, wc, w_words, w_scales, b):
    x_ = mxq(f64(x), 0, "e4m3")
    wx_ = mxq(f64(wx), 0, "e4m3")
    c_ = mxq(f64(c), 0, "e5m2")
    wc_ = mxq(f64(wc), 0, "e4m3")
    w_ = unpack_weight(w_words, w_scales, "e2m1")
    h_ = mxq((wx_.T @ x_) * (wc_.T @ c_), 0, "e4m3")
    y = h_.T @ w_
    return gelu(y + f64(b)[None, :])

@@ -1,0 +1,208 @@
+from contextlib import ExitStack
+
+import concourse.mybir as mybir
+from concourse.masks import make_identity
+
+K, L, R, M, T = 512, 512, 1024, 1024, 1024
+FLOPS = 2 * K * R * T + 2 * L * R * T + 2 * R * M * T
+
+F32 = mybir.dt.float32
+BF16 = mybir.dt.bfloat16
+U32 = mybir.dt.uint32
+I32 = mybir.dt.int32
+U8 = mybir.dt.uint8
+E4M3 = mybir.dt.float8_e4m3fn_x4
+E5M2 = mybir.dt.float8_e5m2_x4
+E2M1 = mybir.dt.float4_e2m1fn_x4
+ALU = mybir.AluOpType
+GELU = mybir.ActivationFunctionType.Gelu_apprx_tanh
+P = 128
+
+PIECES = {'wc0': [512], 'c0': [512], 'wc1': [512], 'wx0': [512], 'x0': [256, 256], 'wx1': [256, 256], 'c1': [512], 'x1': [256, 256]}
+
+SCHEDULE = (
+    "Lwc0_0 Lc0_0 Lwx0_0 Lx0_0 Lwc1_0 Lx0_1 Lwx1_0 Lwx1_1 Lw0 Lc1_0 Ls Lw1 Lx1_0 Lx1_1 act cwc0_0:V "
+    "cwc0_1:S qwc0_0 qwc0_1 bias0 bias1 cc0_01:V cc0_3:S cc0_2:V qc0_0123 pc000 pc001 pc002 pc003 "
+    "cwx0_0:V cwx0_1:S qwx0_0 cp000:V qwx0_1 cx0_01:S qx0_01 cp001:V cp002:S cp003:S px00 px01 cwc1_0:V "
+    "cwc1_1:S qwc1_0 pc100 pc101 M00 M01 qwc1_1 pc102 pc103 cx0_23:S cwx1_0:V qx0_23 px02 px03 cwx1_1:V "
+    "cp100:S cp101:S cwx1_2:V cwx1_3:S qwx1_0 qwx1_1 cp102:S cp103:S M02 M03 px10 px11 px12 px13 cc1_01:S "
+    "cc1_23:S M10 H00123 H10 y00 y01 M11 M12 H11 y10 y11 M13 qc1_0123 pc010 pc011 A00:V H123 A01:V pc012 "
+    "y20 y21 cx1_01:S cx1_23:S cp010:S g00 S00 cp011:S A10:V A11:V pc013 pc110 y30 y31 cp012:S cp013:S "
+    "A20:V A21:V pc111 pc112 qx1_01 qx1_23 px04 px05 cp110:S g01 S01 cp111:S pc113 px06 A30:V A31:V px07 "
+    "px14 cp112:S cp113:S M04 M05 px15 px16 M06 M07 px17 g10 S10 g11 S11 g20 S20 g21 S21 g30 S30 g31 S31 "
+    "M14 H04567 H14 y40 y41 M15 M16 H15 y50 y51 M17 H16 y60 y61 A40:V A41:V H17 y70 y71 g40 S40 g41 S41 "
+    "A50:V A51:V g50 S50 g51 S51 A60:V A61:V g60 S60 g61 S61 A70:V A71:V g70 S70 g71 S71 "
+)
+
+
+def tile_mix_bilin_tm_gelu_kernel(tc, x, wx, c, wc, w_words, w_scales, b, out):
+    nc = tc.nc
+    src = {"x": x, "c": c, "wx": wx, "wc": wc}
+    with ExitStack() as ctx:
+        sb = ctx.enter_context(tc.tile_pool(name="sb", bufs=1))
+        ps = ctx.enter_context(tc.psum_pool(name="ps", bufs=1))
+        banks = [ps.tile([P, 512], F32, name="bank%d" % i) for i in range(8)]
+        free = list(range(8))
+        held = {}
+
+        raw, rawcol, bf, codes, scales = {}, {}, {}, {}, {}
+        for tn, cols in PIECES.items():
+            c0 = 0
+            for i, w in enumerate(cols):
+                raw[(tn, i)] = sb.tile([P, 4, w], F32, name="raw_%s_%d" % (tn, i), align_bytes=64)
+                rawcol[(tn, i)] = (c0, w)
+                c0 += w
+            bf[tn] = sb.tile([P, 2048], BF16, name="bf_" + tn, align_bytes=64)
+            codes[tn] = sb.tile([P, 512], U32, name="codes_" + tn, align_bytes=64)
+            scales[tn] = sb.tile([P, 512], U8, name="scales_" + tn, align_bytes=64)
+        pcs = {(a, h): sb.tile([P, 4, 512], F32, name="pcs%d%d" % (a, h), align_bytes=64) for a in range(2) for h in range(2)}
+        hb = [sb.tile([P, 4 * T], BF16, name="hb%d" % a, align_bytes=64) for a in range(2)]
+        hq = [sb.tile([P, T], U32, name="hq%d" % a, align_bytes=64) for a in range(2)]
+        hs = [sb.tile([P, T], U8, name="hs%d" % a, align_bytes=64) for a in range(2)]
+        res = [sb.tile([P, M], F32, name="res%d" % t, align_bytes=64) for t in range(8)]
+        wt = [sb.tile([P, 2, 1024], U8, name="wt%d" % n, align_bytes=64) for n in range(2)]
+        wplane = sb.tile([P, 2, M], U8, name="wplane", align_bytes=64)
+        bcol = sb.tile([P, 8], F32, name="bcol", align_bytes=64)
+        bias = sb.tile([P, M], F32, name="bias", align_bytes=64)
+        ident = sb.tile([P, P], F32, name="ident", align_bytes=64)
+        warm = sb.tile([P, 2], F32, name="warm", align_bytes=64)
+
+        def take(key):
+            held[key] = free.pop(0)
+            return banks[held[key]]
+
+        def give(key):
+            i = held.pop(key)
+            free.append(i)
+            return banks[i]
+
+        def piece(tn, col):
+            for i in range(len(PIECES[tn])):
+                c0, w = rawcol[(tn, i)]
+                if c0 <= col < c0 + w:
+                    return raw[(tn, i)], col - c0
+
+        def cast(eng, dst, s):
+            if eng == "V":
+                nc.vector.tensor_copy(out=dst, in_=s)
+            elif eng == "S":
+                nc.scalar.copy(out=dst, in_=s)
+            else:
+                nc.gpsimd.tensor_scalar(out=dst, in0=s, scalar1=1.0, scalar2=0.0, op0=ALU.mult, op1=ALU.add)
+
+        def mx(dst, l, ls, r, rs, start=True, stop=True):
+            nc.tensor.matmul_mx(out=dst, lhsT=l, lhsT_scale=ls, rhs=r, rhs_scale=rs, start=start, stop=stop)
+
+        ctx.enter_context(tc.manual_schedule())
+        nc.scalar.dma_start(out=bcol[:], in_=b.rearrange("(p m) -> p m", m=8))
+        nc.vector.memset(warm[:, 0:1], 0.0)
+        make_identity(nc, ident[:])
+        nc.vector.memset(wplane[:].rearrange("p a n -> p (a n)").bitcast(U32), 0)
+
+        for tok in SCHEDULE.split():
+            parts = tok.split(":")
+            n = parts[0]
+            eng = parts[1] if len(parts) > 1 else ""
+            if n == "act":
+                nc.scalar.activation(out=warm[:, 1:2], in_=warm[:, 0:1], func=GELU)
+            elif n.startswith("bias"):
+                u = int(n[4])
+                bk = take(n)
+                for m in range(4):
+                    nc.tensor.transpose(bk[:, m * P:(m + 1) * P], bcol[:, 4 * u + m:4 * u + m + 1].to_broadcast([P, P]), ident[:])
+                give(n)
+                nc.scalar.copy(out=bias[:].rearrange("q (p m) -> q p m", m=8)[:, :, 4 * u:4 * u + 4],
+                               in_=bk[:].rearrange("q (m p) -> q p m", m=4))
+            elif n == "Ls":
+                for q in range(4):
+                    nc.sync.dma_start(out=wplane[32 * q:32 * q + 4, :, :].bitcast(I32),
+                                      in_=w_scales[:, 4 * q:4 * q + 4, :].rearrange("a q n -> q a n").bitcast(I32))
+            elif n in ("Lw0", "Lw1"):
+                h = int(n[2])
+                nc.sync.dma_start(out=wt[h][:].bitcast(I32),
+                                  in_=w_words[:, :, 1024 * h:1024 * (h + 1)].rearrange("a p n -> p a n").bitcast(I32))
+            elif n[0] == "L":
+                tn, i = n[1:].split("_")
+                c0, w = rawcol[(tn, int(i))]
+                c0 += 512 * int(tn[-1])
+                nc.sync.dma_start(out=raw[(tn, int(i))][:],
+                                  in_=src[tn[:-1]][:, c0:c0 + w].rearrange("(p j) w -> p j w", j=4))
+            elif n.startswith("cp"):
+                a, h, j = int(n[2]), int(n[3]), int(n[4])
+                bk = give("pc" + n[2:])
+                if eng == "S":
+                    nc.scalar.copy(out=pcs[(a, h)][:, j, :], in_=bk[:])
+                else:
+                    nc.vector.tensor_copy(out=pcs[(a, h)][:, j, :], in_=bk[:])
+            elif n[0] == "c":
+                tn, s = n[1:].split("_")
+                if tn[0] == "w":
+                    mh, tp = divmod(int(s), 2)
+                    r = raw[(tn, mh)]
+                    mw = rawcol[(tn, mh)][1] // 4
+                    dst = bf[tn][:].rearrange("p (t m j) -> p m j t", t=4, j=4)[:, mw * mh:mw * (mh + 1), :, 2 * tp:2 * tp + 2]
+                    sv = r[:].rearrange("p j (m t) -> p m j t", t=4)[:, :, :, 2 * tp:2 * tp + 2]
+                else:
+                    s0, ns = int(s[0]), len(s)
+                    r, off = piece(tn, P * s0)
+                    dst = bf[tn][:, 512 * s0:512 * (s0 + ns)].rearrange("p (c i j) -> p c j i", i=4, j=4)
+                    sv = r[:, :, off:off + P * ns].rearrange("p j (c i) -> p c j i", i=4)
+                cast(eng, dst, sv)
+            elif n[0] == "q":
+                tn, s = n[1:].split("_")
+                w = 256 if tn[0] == "w" else P
+                c0, c1 = w * int(s[0]), w * (int(s[0]) + len(s))
+                nc.vector.quantize_mx(out=codes[tn][:, c0:c1].bitcast(E5M2 if tn[0] == "c" else E4M3),
+                                      scales=scales[tn][:, c0:c1], in_=bf[tn][:, 4 * c0:4 * c1])
+            elif n.startswith("pc"):
+                a, h, j = n[2], n[3], int(n[4])
+                bk = take(n)
+                js = slice(P * j, P * (j + 1))
+                mx(bk[:], codes["wc" + a][:, js].bitcast(E4M3), scales["wc" + a][:, js],
+                   codes["c" + h][:].bitcast(E5M2), scales["c" + h][:])
+            elif n.startswith("px"):
+                a, t = n[2], int(n[3])
+                bk = take(n)
+                xn = "x%d" % (t // 4)
+                ts = slice(P * (t % 4), P * (t % 4 + 1))
+                for j in range(4):
+                    js = slice(P * j, P * (j + 1))
+                    mx(bk[:, js], codes["wx" + a][:, js].bitcast(E4M3), scales["wx" + a][:, js],
+                       codes[xn][:, ts].bitcast(E4M3), scales[xn][:, ts])
+            elif n[0] == "M":
+                a, t = int(n[1]), int(n[2])
+                bk = give("px" + n[1:])
+                ts = slice(P * (t % 4), P * (t % 4 + 1))
+                nc.vector.tensor_tensor(out=hb[a][:, 512 * t:512 * (t + 1)].rearrange("p (c i j) -> p c j i", i=4, j=4),
+                                        in0=bk[:].rearrange("p (j c i) -> p c j i", j=4, i=4),
+                                        in1=pcs[(a, t // 4)][:, :, ts].rearrange("p j (c i) -> p c j i", i=4),
+                                        op=ALU.mult)
+            elif n[0] == "H":
+                a, c0, c1 = int(n[1]), P * int(n[2]), P * (int(n[-1]) + 1)
+                nc.vector.quantize_mx(out=hq[a][:, c0:c1].bitcast(E4M3), scales=hs[a][:, c0:c1], in_=hb[a][:, 4 * c0:4 * c1])
+            elif n[0] == "y":
+                t, h = int(n[1]), int(n[2])
+                bk = take(n)
+                for a in range(2):
+                    mx(bk[:], hq[a][:, P * t:P * (t + 1)].bitcast(E4M3), hs[a][:, P * t:P * (t + 1)],
+                       wt[h][:, a, :].bitcast(E2M1), wplane[:, a, 512 * h:512 * (h + 1)], start=(a == 0), stop=(a == 1))
+            elif n[0] == "A":
+                t, h = int(n[1]), int(n[2])
+                bk = give("y" + n[1:])
+                ns = slice(512 * h, 512 * (h + 1))
+                if eng == "V":
+                    nc.vector.tensor_tensor(out=res[t][:, ns], in0=bk[:], in1=bias[:, ns], op=ALU.add)
+                else:
+                    nc.scalar.copy(out=res[t][:, ns], in_=bk[:])
+            elif n[0] == "G":
+                t, h = int(n[1]), int(n[2])
+                ns = slice(512 * h, 512 * (h + 1))
+                nc.gpsimd.tensor_tensor(out=res[t][:, ns], in0=res[t][:, ns], in1=bias[:, ns], op=ALU.add)
+            elif n[0] == "g":
+                t, h = int(n[1]), int(n[2])
+                ns = slice(512 * h, 512 * (h + 1))
+                nc.scalar.activation(out=res[t][:, ns], in_=res[t][:, ns], func=GELU)
+            elif n[0] == "S":
+                t, h = int(n[1]), int(n[2])
+                ns = slice(512 * h, 512 * (h + 1))
+                nc.sync.dma_start(out=out[P * t:P * (t + 1), ns], in_=res[t][:, ns])

@@ -16,193 +16,296 @@ E5M2 = mybir.dt.float8_e5m2_x4
 E2M1 = mybir.dt.float4_e2m1fn_x4
 ALU = mybir.AluOpType
 GELU = mybir.ActivationFunctionType.Gelu_apprx_tanh
+
 P = 128
+PACK = 4
+HALF = 512
+QUARTER = HALF // 2
+RUN = 4
+BANKS = 8
 
-PIECES = {'wc0': [512], 'c0': [512], 'wc1': [512], 'wx0': [512], 'x0': [256, 256], 'wx1': [256, 256], 'c1': [512], 'x1': [256, 256]}
+PIECES = {("wc", 0): 1, ("c", 0): 1, ("wx", 0): 1, ("x", 0): 2, ("wc", 1): 2, ("wx", 1): 2, ("c", 1): 1, ("x", 1): 2}
 
-SCHEDULE = (
-    "Lwc0_0 Lc0_0 Lwx0_0 Lx0_0 Lwc1_0 Lx0_1 Lwx1_0 Lwx1_1 Lw0 Lc1_0 Ls Lw1 Lx1_0 Lx1_1 act cwc0_0:V "
-    "cwc0_1:S qwc0_0 qwc0_1 bias0 bias1 cc0_01:V cc0_3:S cc0_2:V qc0_0123 pc000 pc001 pc002 pc003 "
-    "cwx0_0:V cwx0_1:S qwx0_0 cp000:V qwx0_1 cx0_01:S qx0_01 cp001:V cp002:S cp003:S px00 px01 cwc1_0:V "
-    "cwc1_1:S qwc1_0 pc100 pc101 M00 M01 qwc1_1 pc102 pc103 cx0_23:S cwx1_0:V qx0_23 px02 px03 cwx1_1:V "
-    "cp100:S cp101:S cwx1_2:V cwx1_3:S qwx1_0 qwx1_1 cp102:S cp103:S M02 M03 px10 px11 px12 px13 cc1_01:S "
-    "cc1_23:S M10 H00123 H10 y00 y01 M11 M12 H11 y10 y11 M13 qc1_0123 pc010 pc011 A00:V H123 A01:V pc012 "
-    "y20 y21 cx1_01:S cx1_23:S cp010:S g00 S00 cp011:S A10:V A11:V pc013 pc110 y30 y31 cp012:S cp013:S "
-    "A20:V A21:V pc111 pc112 qx1_01 qx1_23 px04 px05 cp110:S g01 S01 cp111:S pc113 px06 A30:V A31:V px07 "
-    "px14 cp112:S cp113:S M04 M05 px15 px16 M06 M07 px17 g10 S10 g11 S11 g20 S20 g21 S21 g30 S30 g31 S31 "
-    "M14 H04567 H14 y40 y41 M15 M16 H15 y50 y51 M17 H16 y60 y61 A40:V A41:V H17 y70 y71 g40 S40 g41 S41 "
-    "A50:V A51:V g50 S50 g51 S51 A60:V A61:V g60 S60 g61 S61 A70:V A71:V g70 S70 g71 S71 "
-)
+
+def span(index, width, count=1):
+    return slice(index * width, (index + count) * width)
 
 
 def tile_mix_bilin_tm_gelu_kernel(tc, x, wx, c, wc, w_words, w_scales, b, out):
     nc = tc.nc
-    src = {"x": x, "c": c, "wx": wx, "wc": wc}
+    source = {"x": x, "c": c, "wx": wx, "wc": wc}
+    on_vector, on_scalar = nc.vector.tensor_copy, nc.scalar.copy
+
     with ExitStack() as ctx:
-        sb = ctx.enter_context(tc.tile_pool(name="sb", bufs=1))
-        ps = ctx.enter_context(tc.psum_pool(name="ps", bufs=1))
-        banks = [ps.tile([P, 512], F32, name="bank%d" % i) for i in range(8)]
-        free = list(range(8))
+        sbuf = ctx.enter_context(tc.tile_pool(name="sbuf", bufs=1))
+        psum = ctx.enter_context(tc.psum_pool(name="psum", bufs=1))
+
+        def keep(name, shape, dtype):
+            return sbuf.tile(shape, dtype, name=name, align_bytes=64)
+
+        raw, rounded, words, plane = {}, {}, {}, {}
+        for half, pieces in PIECES.items():
+            name = "%s%d" % half
+            raw[half] = [keep("raw_%s_%d" % (name, i), [P, PACK, HALF // pieces], F32) for i in range(pieces)]
+            rounded[half] = keep("rounded_" + name, [P, PACK * HALF], BF16)
+            words[half] = keep("words_" + name, [P, HALF], U32)
+            plane[half] = keep("plane_" + name, [P, HALF], U8)
+        pc = {(a, th): keep("pc%d%d" % (a, th), [P, PACK, HALF], F32) for a in range(2) for th in range(2)}
+        for a in range(2):
+            rounded[("h", a)] = keep("rounded_h%d" % a, [P, PACK * T], BF16)
+            words[("h", a)] = keep("words_h%d" % a, [P, T], U32)
+            plane[("h", a)] = keep("plane_h%d" % a, [P, T], U8)
+        result = [keep("result%d" % t, [P, M], F32) for t in range(T // P)]
+        w_codes = [keep("w_codes%d" % nh, [P, 2, 2 * HALF], U8) for nh in range(2)]
+        w_plane = keep("w_plane", [P, 2, M], U8)
+        b_rows = keep("b_rows", [P, M // P], F32)
+        bias = keep("bias", [P, M], F32)
+        identity = keep("identity", [P, P], F32)
+        warm = keep("warm", [P, 2], F32)
+
+        free = [psum.tile([P, HALF], F32, name="bank%d" % i) for i in range(BANKS)]
         held = {}
 
-        raw, rawcol, bf, codes, scales = {}, {}, {}, {}, {}
-        for tn, cols in PIECES.items():
-            c0 = 0
-            for i, w in enumerate(cols):
-                raw[(tn, i)] = sb.tile([P, 4, w], F32, name="raw_%s_%d" % (tn, i), align_bytes=64)
-                rawcol[(tn, i)] = (c0, w)
-                c0 += w
-            bf[tn] = sb.tile([P, 2048], BF16, name="bf_" + tn, align_bytes=64)
-            codes[tn] = sb.tile([P, 512], U32, name="codes_" + tn, align_bytes=64)
-            scales[tn] = sb.tile([P, 512], U8, name="scales_" + tn, align_bytes=64)
-        pcs = {(a, h): sb.tile([P, 4, 512], F32, name="pcs%d%d" % (a, h), align_bytes=64) for a in range(2) for h in range(2)}
-        hb = [sb.tile([P, 4 * T], BF16, name="hb%d" % a, align_bytes=64) for a in range(2)]
-        hq = [sb.tile([P, T], U32, name="hq%d" % a, align_bytes=64) for a in range(2)]
-        hs = [sb.tile([P, T], U8, name="hs%d" % a, align_bytes=64) for a in range(2)]
-        res = [sb.tile([P, M], F32, name="res%d" % t, align_bytes=64) for t in range(8)]
-        wt = [sb.tile([P, 2, 1024], U8, name="wt%d" % n, align_bytes=64) for n in range(2)]
-        wplane = sb.tile([P, 2, M], U8, name="wplane", align_bytes=64)
-        bcol = sb.tile([P, 8], F32, name="bcol", align_bytes=64)
-        bias = sb.tile([P, M], F32, name="bias", align_bytes=64)
-        ident = sb.tile([P, P], F32, name="ident", align_bytes=64)
-        warm = sb.tile([P, 2], F32, name="warm", align_bytes=64)
-
-        def take(key):
+        def take_bank(key):
             held[key] = free.pop(0)
-            return banks[held[key]]
+            return held[key]
 
-        def give(key):
-            i = held.pop(key)
-            free.append(i)
-            return banks[i]
+        def return_bank(key):
+            free.append(held.pop(key))
 
-        def piece(tn, col):
-            for i in range(len(PIECES[tn])):
-                c0, w = rawcol[(tn, i)]
-                if c0 <= col < c0 + w:
-                    return raw[(tn, i)], col - c0
+        def load(half, i=0):
+            width = raw[half][i].shape[2]
+            first = half[1] * HALF + i * width
+            rows = source[half[0]][:, first:first + width].rearrange("(p j) w -> p j w", j=PACK)
+            nc.sync.dma_start(out=raw[half][i][:], in_=rows)
 
-        def cast(eng, dst, s):
-            if eng == "V":
-                nc.vector.tensor_copy(out=dst, in_=s)
-            elif eng == "S":
-                nc.scalar.copy(out=dst, in_=s)
-            else:
-                nc.gpsimd.tensor_scalar(out=dst, in0=s, scalar1=1.0, scalar2=0.0, op0=ALU.mult, op1=ALU.add)
+        def load_w_scales():
+            for quad in range(4):
+                rows = w_scales[:, span(quad, 4), :].rearrange("a q n -> q a n")
+                nc.sync.dma_start(out=w_plane[32 * quad:32 * quad + 4, :, :].bitcast(I32), in_=rows.bitcast(I32))
 
-        def mx(dst, l, ls, r, rs, start=True, stop=True):
-            nc.tensor.matmul_mx(out=dst, lhsT=l, lhsT_scale=ls, rhs=r, rhs_scale=rs, start=start, stop=stop)
+        def load_w_codes(nh):
+            rows = w_words[:, :, span(nh, 2 * HALF)].rearrange("a p n -> p a n")
+            nc.sync.dma_start(out=w_codes[nh][:].bitcast(I32), in_=rows.bitcast(I32))
+
+        def spread_bias(u):
+            bank = take_bank("bias")
+            for m in range(4):
+                column = b_rows[:, span(4 * u + m, 1)].to_broadcast([P, P])
+                nc.tensor.transpose(bank[:, span(m, P)], column, identity[:])
+            nc.scalar.copy(out=bias[:].rearrange("q (p m) -> q p m", p=P)[:, :, span(u, 4)],
+                           in_=bank[:].rearrange("q (m p) -> q p m", p=P))
+            return_bank("bias")
+
+        def round_weight(copy, half, pair, i=0):
+            count = raw[half][i].shape[2] // PACK
+            dst = rounded[half][:].rearrange("p (s m j) -> p m j s", s=PACK, j=PACK)
+            src = raw[half][i][:].rearrange("p j (m s) -> p m j s", s=PACK)
+            copy(out=dst[:, span(i, count), :, span(pair, 2)], in_=src[:, :, :, span(pair, 2)])
+
+        def round_stream(copy, half, first, count):
+            i, start = divmod(first * P, raw[half][0].shape[2])
+            dst = rounded[half][:, span(first, PACK * P, count)].rearrange("p (u v j) -> p u j v", v=RUN, j=PACK)
+            src = raw[half][i][:, :, start:start + count * P].rearrange("p j (u v) -> p u j v", v=RUN)
+            copy(out=dst, in_=src)
+
+        def quantise(half, first, count):
+            cols = span(first, P, count)
+            nc.vector.quantize_mx(out=words[half][:, cols].bitcast(E5M2 if half[0] == "c" else E4M3),
+                                  scales=plane[half][:, cols], in_=rounded[half][:, span(first, PACK * P, count)])
+
+        def project_c(a, th, j):
+            nc.tensor.matmul_mx(out=take_bank(("pc", a, th, j))[:],
+                                lhsT=words[("wc", a)][:, span(j, P)].bitcast(E4M3), lhsT_scale=plane[("wc", a)][:, span(j, P)],
+                                rhs=words[("c", th)][:].bitcast(E5M2), rhs_scale=plane[("c", th)][:], start=True, stop=True)
+
+        def drain_c(a, th, j, copy=on_scalar):
+            copy(out=pc[(a, th)][:, j, :], in_=held[("pc", a, th, j)][:])
+            return_bank(("pc", a, th, j))
+
+        def project_x(a, t):
+            bank = take_bank(("px", a, t))
+            th, cols = t // 4, span(t % 4, P)
+            for j in range(PACK):
+                nc.tensor.matmul_mx(out=bank[:, span(j, P)],
+                                    lhsT=words[("wx", a)][:, span(j, P)].bitcast(E4M3), lhsT_scale=plane[("wx", a)][:, span(j, P)],
+                                    rhs=words[("x", th)][:, cols].bitcast(E4M3), rhs_scale=plane[("x", th)][:, cols],
+                                    start=True, stop=True)
+
+        def multiply(a, t):
+            nc.vector.tensor_tensor(
+                out=rounded[("h", a)][:, span(t, PACK * P)].rearrange("p (u v j) -> p u j v", v=RUN, j=PACK),
+                in0=held[("px", a, t)][:].rearrange("p (j u v) -> p u j v", j=PACK, v=RUN),
+                in1=pc[(a, t // 4)][:, :, span(t % 4, P)].rearrange("p j (u v) -> p u j v", v=RUN),
+                op=ALU.mult)
+            return_bank(("px", a, t))
+
+        def project_out(t, nh):
+            bank = take_bank(("y", t, nh))
+            for a in range(2):
+                nc.tensor.matmul_mx(out=bank[:],
+                                    lhsT=words[("h", a)][:, span(t, P)].bitcast(E4M3), lhsT_scale=plane[("h", a)][:, span(t, P)],
+                                    rhs=w_codes[nh][:, a, :].bitcast(E2M1), rhs_scale=w_plane[:, a, span(nh, HALF)],
+                                    start=(a == 0), stop=(a == 1))
+
+        def add_bias(t, nh, first=0, width=HALF):
+            cols = slice(nh * HALF + first, nh * HALF + first + width)
+            nc.vector.tensor_tensor(out=result[t][:, cols], in0=held[("y", t, nh)][:, first:first + width],
+                                    in1=bias[:, cols], op=ALU.add)
+            if first + width == HALF:
+                return_bank(("y", t, nh))
+
+        def finish(t, first, width):
+            cols = slice(first, first + width)
+            nc.scalar.activation(out=result[t][:, cols], in_=result[t][:, cols], func=GELU)
+            nc.sync.dma_start(out=out[span(t, P), cols], in_=result[t][:, cols])
 
         ctx.enter_context(tc.manual_schedule())
-        nc.scalar.dma_start(out=bcol[:], in_=b.rearrange("(p m) -> p m", m=8))
-        nc.vector.memset(warm[:, 0:1], 0.0)
-        make_identity(nc, ident[:])
-        nc.vector.memset(wplane[:].rearrange("p a n -> p (a n)").bitcast(U32), 0)
 
-        for tok in SCHEDULE.split():
-            parts = tok.split(":")
-            n = parts[0]
-            eng = parts[1] if len(parts) > 1 else ""
-            if n == "act":
-                nc.scalar.activation(out=warm[:, 1:2], in_=warm[:, 0:1], func=GELU)
-            elif n.startswith("bias"):
-                u = int(n[4])
-                bk = take(n)
-                for m in range(4):
-                    nc.tensor.transpose(bk[:, m * P:(m + 1) * P], bcol[:, 4 * u + m:4 * u + m + 1].to_broadcast([P, P]), ident[:])
-                give(n)
-                nc.scalar.copy(out=bias[:].rearrange("q (p m) -> q p m", m=8)[:, :, 4 * u:4 * u + 4],
-                               in_=bk[:].rearrange("q (m p) -> q p m", m=4))
-            elif n == "Ls":
-                for q in range(4):
-                    nc.sync.dma_start(out=wplane[32 * q:32 * q + 4, :, :].bitcast(I32),
-                                      in_=w_scales[:, 4 * q:4 * q + 4, :].rearrange("a q n -> q a n").bitcast(I32))
-            elif n in ("Lw0", "Lw1"):
-                h = int(n[2])
-                nc.sync.dma_start(out=wt[h][:].bitcast(I32),
-                                  in_=w_words[:, :, 1024 * h:1024 * (h + 1)].rearrange("a p n -> p a n").bitcast(I32))
-            elif n[0] == "L":
-                tn, i = n[1:].split("_")
-                c0, w = rawcol[(tn, int(i))]
-                c0 += 512 * int(tn[-1])
-                nc.sync.dma_start(out=raw[(tn, int(i))][:],
-                                  in_=src[tn[:-1]][:, c0:c0 + w].rearrange("(p j) w -> p j w", j=4))
-            elif n.startswith("cp"):
-                a, h, j = int(n[2]), int(n[3]), int(n[4])
-                bk = give("pc" + n[2:])
-                if eng == "S":
-                    nc.scalar.copy(out=pcs[(a, h)][:, j, :], in_=bk[:])
-                else:
-                    nc.vector.tensor_copy(out=pcs[(a, h)][:, j, :], in_=bk[:])
-            elif n[0] == "c":
-                tn, s = n[1:].split("_")
-                if tn[0] == "w":
-                    mh, tp = divmod(int(s), 2)
-                    r = raw[(tn, mh)]
-                    mw = rawcol[(tn, mh)][1] // 4
-                    dst = bf[tn][:].rearrange("p (t m j) -> p m j t", t=4, j=4)[:, mw * mh:mw * (mh + 1), :, 2 * tp:2 * tp + 2]
-                    sv = r[:].rearrange("p j (m t) -> p m j t", t=4)[:, :, :, 2 * tp:2 * tp + 2]
-                else:
-                    s0, ns = int(s[0]), len(s)
-                    r, off = piece(tn, P * s0)
-                    dst = bf[tn][:, 512 * s0:512 * (s0 + ns)].rearrange("p (c i j) -> p c j i", i=4, j=4)
-                    sv = r[:, :, off:off + P * ns].rearrange("p j (c i) -> p c j i", i=4)
-                cast(eng, dst, sv)
-            elif n[0] == "q":
-                tn, s = n[1:].split("_")
-                w = 256 if tn[0] == "w" else P
-                c0, c1 = w * int(s[0]), w * (int(s[0]) + len(s))
-                nc.vector.quantize_mx(out=codes[tn][:, c0:c1].bitcast(E5M2 if tn[0] == "c" else E4M3),
-                                      scales=scales[tn][:, c0:c1], in_=bf[tn][:, 4 * c0:4 * c1])
-            elif n.startswith("pc"):
-                a, h, j = n[2], n[3], int(n[4])
-                bk = take(n)
-                js = slice(P * j, P * (j + 1))
-                mx(bk[:], codes["wc" + a][:, js].bitcast(E4M3), scales["wc" + a][:, js],
-                   codes["c" + h][:].bitcast(E5M2), scales["c" + h][:])
-            elif n.startswith("px"):
-                a, t = n[2], int(n[3])
-                bk = take(n)
-                xn = "x%d" % (t // 4)
-                ts = slice(P * (t % 4), P * (t % 4 + 1))
-                for j in range(4):
-                    js = slice(P * j, P * (j + 1))
-                    mx(bk[:, js], codes["wx" + a][:, js].bitcast(E4M3), scales["wx" + a][:, js],
-                       codes[xn][:, ts].bitcast(E4M3), scales[xn][:, ts])
-            elif n[0] == "M":
-                a, t = int(n[1]), int(n[2])
-                bk = give("px" + n[1:])
-                ts = slice(P * (t % 4), P * (t % 4 + 1))
-                nc.vector.tensor_tensor(out=hb[a][:, 512 * t:512 * (t + 1)].rearrange("p (c i j) -> p c j i", i=4, j=4),
-                                        in0=bk[:].rearrange("p (j c i) -> p c j i", j=4, i=4),
-                                        in1=pcs[(a, t // 4)][:, :, ts].rearrange("p j (c i) -> p c j i", i=4),
-                                        op=ALU.mult)
-            elif n[0] == "H":
-                a, c0, c1 = int(n[1]), P * int(n[2]), P * (int(n[-1]) + 1)
-                nc.vector.quantize_mx(out=hq[a][:, c0:c1].bitcast(E4M3), scales=hs[a][:, c0:c1], in_=hb[a][:, 4 * c0:4 * c1])
-            elif n[0] == "y":
-                t, h = int(n[1]), int(n[2])
-                bk = take(n)
-                for a in range(2):
-                    mx(bk[:], hq[a][:, P * t:P * (t + 1)].bitcast(E4M3), hs[a][:, P * t:P * (t + 1)],
-                       wt[h][:, a, :].bitcast(E2M1), wplane[:, a, 512 * h:512 * (h + 1)], start=(a == 0), stop=(a == 1))
-            elif n[0] == "A":
-                t, h = int(n[1]), int(n[2])
-                bk = give("y" + n[1:])
-                ns = slice(512 * h, 512 * (h + 1))
-                if eng == "V":
-                    nc.vector.tensor_tensor(out=res[t][:, ns], in0=bk[:], in1=bias[:, ns], op=ALU.add)
-                else:
-                    nc.scalar.copy(out=res[t][:, ns], in_=bk[:])
-            elif n[0] == "G":
-                t, h = int(n[1]), int(n[2])
-                ns = slice(512 * h, 512 * (h + 1))
-                nc.gpsimd.tensor_tensor(out=res[t][:, ns], in0=res[t][:, ns], in1=bias[:, ns], op=ALU.add)
-            elif n[0] == "g":
-                t, h = int(n[1]), int(n[2])
-                ns = slice(512 * h, 512 * (h + 1))
-                nc.scalar.activation(out=res[t][:, ns], in_=res[t][:, ns], func=GELU)
-            elif n[0] == "S":
-                t, h = int(n[1]), int(n[2])
-                ns = slice(512 * h, 512 * (h + 1))
-                nc.sync.dma_start(out=out[P * t:P * (t + 1), ns], in_=res[t][:, ns])
+        nc.scalar.dma_start(out=b_rows[:], in_=b.rearrange("(p m) -> p m", p=P))
+        nc.vector.memset(warm[:, 0:1], 0.0)
+        make_identity(nc, identity[:])
+        nc.vector.memset(w_plane[:].rearrange("p a n -> p (a n)").bitcast(U32), 0)
+
+        for half in (("wc", 0), ("c", 0), ("wx", 0), ("x", 0), ("wc", 1), ("wx", 1), ("c", 1)):
+            for i in range(PIECES[half]):
+                load(half, i)
+        load_w_scales()
+        for nh in range(2):
+            load_w_codes(nh)
+        for i in range(2):
+            load(("x", 1), i)
+
+        nc.scalar.activation(out=warm[:, 1:2], in_=warm[:, 0:1], func=GELU)
+
+        round_weight(on_vector, ("wc", 0), 0)
+        round_weight(on_scalar, ("wc", 0), 1)
+        quantise(("wc", 0), 0, 2)
+        for u in range(2):
+            spread_bias(u)
+        round_stream(on_vector, ("c", 0), 0, 2)
+        quantise(("wc", 0), 2, 2)
+        round_stream(on_scalar, ("c", 0), 2, 2)
+        quantise(("c", 0), 0, 4)
+        for j in range(PACK):
+            project_c(0, 0, j)
+        round_weight(on_vector, ("wx", 0), 0)
+        round_weight(on_scalar, ("wx", 0), 1)
+        quantise(("wx", 0), 0, 2)
+        round_stream(on_vector, ("x", 0), 0, 2)
+        quantise(("wx", 0), 2, 2)
+        quantise(("x", 0), 0, 2)
+        round_stream(on_vector, ("x", 0), 2, 2)
+        quantise(("x", 0), 2, 2)
+        for j in range(PACK):
+            drain_c(0, 0, j)
+        for t in range(4):
+            project_x(0, t)
+        for t in range(4):
+            multiply(0, t)
+
+        for i in range(2):
+            for pair in range(2):
+                round_weight(on_scalar, ("wc", 1), pair, i)
+        for pair in range(2):
+            quantise(("wc", 1), 2 * pair, 2)
+        quantise(("h", 0), 0, 4)
+        for j in range(PACK):
+            project_c(1, 0, j)
+        for i, copy in enumerate((on_scalar, on_vector)):
+            for pair in range(2):
+                round_weight(copy, ("wx", 1), pair, i)
+        for pair in range(2):
+            quantise(("wx", 1), 2 * pair, 2)
+        for j in range(PACK):
+            drain_c(1, 0, j, on_vector if j == PACK - 1 else on_scalar)
+
+        for t in range(4):
+            project_x(1, t)
+        for first in (0, 2):
+            round_stream(on_scalar, ("c", 1), first, 2)
+        multiply(1, 0)
+        multiply(1, 1)
+        quantise(("h", 1), 0, 1)
+        multiply(1, 2)
+        quantise(("h", 1), 1, 1)
+        for t in range(2):
+            for nh in range(2):
+                project_out(t, nh)
+        multiply(1, 3)
+        quantise(("c", 1), 0, 4)
+        quantise(("h", 1), 2, 2)
+        project_c(0, 1, 0)
+        add_bias(0, 0)
+        add_bias(0, 1)
+        project_out(2, 0)
+        project_c(0, 1, 1)
+        project_c(0, 1, 2)
+        project_out(2, 1)
+        add_bias(1, 0)
+        add_bias(1, 1)
+        project_out(3, 0)
+        project_out(3, 1)
+        round_stream(on_scalar, ("x", 1), 0, 2)
+        drain_c(0, 1, 0)
+        round_stream(on_scalar, ("x", 1), 2, 2)
+        drain_c(0, 1, 1)
+        drain_c(0, 1, 2)
+        quantise(("x", 1), 0, 2)
+        add_bias(2, 0)
+        add_bias(2, 1)
+        project_x(0, 4)
+        project_c(0, 1, 3)
+        project_c(1, 1, 0)
+        project_c(1, 1, 1)
+        drain_c(0, 1, 3)
+        project_c(1, 1, 2)
+        quantise(("x", 1), 2, 2)
+        add_bias(3, 0)
+        add_bias(3, 1)
+        for t in range(5, 8):
+            project_x(0, t)
+        drain_c(1, 1, 0)
+        drain_c(1, 1, 1)
+        project_c(1, 1, 3)
+        drain_c(1, 1, 2)
+        drain_c(1, 1, 3)
+
+        for first in (4, 6):
+            multiply(0, first)
+            multiply(0, first + 1)
+            project_x(1, first)
+            project_x(1, first + 1)
+        for t in range(4):
+            finish(t, 0, M)
+        multiply(1, 4)
+        quantise(("h", 0), 4, 4)
+        quantise(("h", 1), 4, 1)
+        project_out(4, 0)
+        project_out(4, 1)
+        multiply(1, 5)
+        for t in (5, 6):
+            multiply(1, t + 1)
+            quantise(("h", 1), t, 1)
+            project_out(t, 0)
+            project_out(t, 1)
+        add_bias(4, 0)
+        add_bias(4, 1)
+        add_bias(5, 0)
+        quantise(("h", 1), 7, 1)
+        project_out(7, 0)
+        project_out(7, 1)
+
+        finish(4, 0, HALF)
+        finish(4, HALF, HALF)
+        add_bias(5, 1)
+        finish(5, 0, HALF)
+        finish(5, HALF, HALF)
+        for nh in range(2):
+            add_bias(6, nh)
+            finish(6, nh * HALF, HALF)
+        add_bias(7, 0)
+        finish(7, 0, HALF)
+        for first in (0, QUARTER):
+            add_bias(7, 1, first, QUARTER)
+            finish(7, HALF + first, QUARTER)

@@ -103,16 +103,22 @@ def tile_mix_bilin_tm_gelu_kernel(tc, x, wx, c, wc, w_words, w_scales, b, out):
             src = raw[half][i][:].rearrange("p j (m s) -> p m j s", s=PACK)
             copy(out=dst[:, span(i, count), :, span(pair, 2)], in_=src[:, :, :, span(pair, 2)])
 
+        def round_last_x():
+            nc.gpsimd.tensor_scalar(out=rounded[("x", 1)][:, span(0, PACK * QUARTER)].rearrange("p (w j) -> p w j", j=PACK),
+                                    in0=raw[("x", 1)][1][:].rearrange("p j w -> p w j"),
+                                    scalar1=1.0, scalar2=0.0, op0=ALU.mult, op1=ALU.add)
+
         def round_stream(copy, half, first, count):
             i, start = divmod(first * P, raw[half][0].shape[2])
             dst = rounded[half][:, span(first, PACK * P, count)].rearrange("p (u v j) -> p u j v", v=RUN, j=PACK)
             src = raw[half][i][:, :, start:start + count * P].rearrange("p j (u v) -> p u j v", v=RUN)
             copy(out=dst, in_=src)
 
-        def quantise(half, first, count):
+        def quantise(half, first, count, read_from=None):
             cols = span(first, P, count)
+            values = rounded[half][:, span(first if read_from is None else read_from, PACK * P, count)]
             nc.vector.quantize_mx(out=words[half][:, cols].bitcast(E5M2 if half[0] == "c" else E4M3),
-                                  scales=plane[half][:, cols], in_=rounded[half][:, span(first, PACK * P, count)])
+                                  scales=plane[half][:, cols], in_=values)
 
         def project_c(a, th, j):
             nc.tensor.matmul_mx(out=take_bank(("pc", a, th, j))[:],
@@ -155,10 +161,24 @@ def tile_mix_bilin_tm_gelu_kernel(tc, x, wx, c, wc, w_words, w_scales, b, out):
             if first + width == HALF:
                 return_bank(("y", t, nh))
 
-        def finish(t, first, width):
+        def drain_out(t, nh):
+            nc.scalar.copy(out=result[t][:, span(nh, HALF)], in_=held[("y", t, nh)][:])
+            return_bank(("y", t, nh))
+
+        def add_bias_gpsimd(t, nh, spare):
+            nc.gpsimd.tensor_tensor(out=spare, in0=result[t][:, span(nh, HALF)], in1=bias[:, span(nh, HALF)], op=ALU.add)
+
+        def gelu(t, first, width, values=None):
             cols = slice(first, first + width)
-            nc.scalar.activation(out=result[t][:, cols], in_=result[t][:, cols], func=GELU)
+            nc.scalar.activation(out=result[t][:, cols], in_=result[t][:, cols] if values is None else values, func=GELU)
+
+        def store(t, first, width):
+            cols = slice(first, first + width)
             nc.sync.dma_start(out=out[span(t, P), cols], in_=result[t][:, cols])
+
+        def finish(t, first, width):
+            gelu(t, first, width)
+            store(t, first, width)
 
         ctx.enter_context(tc.manual_schedule())
 
@@ -233,51 +253,65 @@ def tile_mix_bilin_tm_gelu_kernel(tc, x, wx, c, wc, w_words, w_scales, b, out):
             for nh in range(2):
                 project_out(t, nh)
         multiply(1, 3)
+        drain_out(0, 0)
         quantise(("c", 1), 0, 4)
         quantise(("h", 1), 2, 2)
+        spare0 = rounded[("h", 1)][:, span(2, PACK * P, 2)].bitcast(F32)
+        add_bias_gpsimd(0, 0, spare0)
         project_c(0, 1, 0)
-        add_bias(0, 0)
-        add_bias(0, 1)
-        project_out(2, 0)
         project_c(0, 1, 1)
-        project_c(0, 1, 2)
-        project_out(2, 1)
-        add_bias(1, 0)
-        add_bias(1, 1)
-        project_out(3, 0)
-        project_out(3, 1)
         round_stream(on_scalar, ("x", 1), 0, 2)
-        drain_c(0, 1, 0)
-        round_stream(on_scalar, ("x", 1), 2, 2)
-        drain_c(0, 1, 1)
-        drain_c(0, 1, 2)
-        quantise(("x", 1), 0, 2)
-        add_bias(2, 0)
-        add_bias(2, 1)
-        project_x(0, 4)
+        add_bias(0, 1)
+        project_c(0, 1, 2)
+        add_bias(1, 0)
         project_c(0, 1, 3)
+        drain_c(0, 1, 0)
+        project_out(2, 0)
+        add_bias(1, 1)
+        drain_c(0, 1, 1)
         project_c(1, 1, 0)
-        project_c(1, 1, 1)
+        quantise(("x", 1), 0, 2)
+        round_last_x()
+        project_out(2, 1)
+        drain_c(0, 1, 2)
+        project_out(3, 0)
         drain_c(0, 1, 3)
-        project_c(1, 1, 2)
-        quantise(("x", 1), 2, 2)
-        add_bias(3, 0)
-        add_bias(3, 1)
-        for t in range(5, 8):
-            project_x(0, t)
+        add_bias(2, 0)
+        project_c(1, 1, 1)
+        project_out(3, 1)
+        add_bias(2, 1)
         drain_c(1, 1, 0)
         drain_c(1, 1, 1)
+        project_x(0, 4)
+        add_bias(3, 0)
+        project_x(0, 5)
+        drain_out(3, 1)
+        quantise(("x", 1), 2, 2, read_from=0)
+        spare3 = rounded[("x", 1)][:, span(0, PACK * QUARTER)].bitcast(F32)
+        add_bias_gpsimd(3, 1, spare3)
+        project_c(1, 1, 2)
         project_c(1, 1, 3)
+        project_x(0, 6)
+        multiply(0, 4)
+        project_x(0, 7)
         drain_c(1, 1, 2)
+        multiply(0, 5)
         drain_c(1, 1, 3)
 
-        for first in (4, 6):
-            multiply(0, first)
-            multiply(0, first + 1)
-            project_x(1, first)
-            project_x(1, first + 1)
-        for t in range(4):
+        project_x(1, 4)
+        project_x(1, 5)
+        multiply(0, 6)
+        multiply(0, 7)
+        project_x(1, 6)
+        project_x(1, 7)
+        gelu(0, 0, HALF, spare0)
+        gelu(0, HALF, HALF)
+        store(0, 0, M)
+        for t in (1, 2):
             finish(t, 0, M)
+        gelu(3, 0, HALF)
+        gelu(3, HALF, HALF, spare3)
+        store(3, 0, M)
         multiply(1, 4)
         quantise(("h", 0), 4, 4)
         quantise(("h", 1), 4, 1)
@@ -291,10 +325,10 @@ def tile_mix_bilin_tm_gelu_kernel(tc, x, wx, c, wc, w_words, w_scales, b, out):
             project_out(t, 1)
         add_bias(4, 0)
         add_bias(4, 1)
-        add_bias(5, 0)
         quantise(("h", 1), 7, 1)
         project_out(7, 0)
         project_out(7, 1)
+        add_bias(5, 0)
 
         finish(4, 0, HALF)
         finish(4, HALF, HALF)

from contextlib import ExitStack

import concourse.mybir as mybir
from concourse.masks import make_identity

K, L, R, M, T = 512, 512, 1024, 1024, 1024
FLOPS = 2 * K * R * T + 2 * L * R * T + 2 * R * M * T

F32 = mybir.dt.float32
BF16 = mybir.dt.bfloat16
U32 = mybir.dt.uint32
I32 = mybir.dt.int32
U8 = mybir.dt.uint8
E4M3 = mybir.dt.float8_e4m3fn_x4
E5M2 = mybir.dt.float8_e5m2_x4
E2M1 = mybir.dt.float4_e2m1fn_x4
ALU = mybir.AluOpType
GELU = mybir.ActivationFunctionType.Gelu_apprx_tanh

P = 128
PACK = 4
HALF = 512
QUARTER = HALF // 2
RUN = 4
BANKS = 8

PIECES = {("wc", 0): 1, ("c", 0): 1, ("wx", 0): 1, ("x", 0): 2, ("wc", 1): 2, ("wx", 1): 2, ("c", 1): 1, ("x", 1): 2}


def span(index, width, count=1):
    return slice(index * width, (index + count) * width)


def tile_mix_bilin_tm_gelu_kernel(tc, x, wx, c, wc, w_words, w_scales, b, out):
    nc = tc.nc
    source = {"x": x, "c": c, "wx": wx, "wc": wc}
    on_vector, on_scalar = nc.vector.tensor_copy, nc.scalar.copy

    with ExitStack() as ctx:
        sbuf = ctx.enter_context(tc.tile_pool(name="sbuf", bufs=1))
        psum = ctx.enter_context(tc.psum_pool(name="psum", bufs=1))

        def keep(name, shape, dtype):
            return sbuf.tile(shape, dtype, name=name, align_bytes=64)

        raw, rounded, words, plane = {}, {}, {}, {}
        for half, pieces in PIECES.items():
            name = "%s%d" % half
            raw[half] = [keep("raw_%s_%d" % (name, i), [P, PACK, HALF // pieces], F32) for i in range(pieces)]
            rounded[half] = keep("rounded_" + name, [P, PACK * HALF], BF16)
            words[half] = keep("words_" + name, [P, HALF], U32)
            plane[half] = keep("plane_" + name, [P, HALF], U8)
        pc = {(a, th): keep("pc%d%d" % (a, th), [P, PACK, HALF], F32) for a in range(2) for th in range(2)}
        for a in range(2):
            rounded[("h", a)] = keep("rounded_h%d" % a, [P, PACK * T], BF16)
            words[("h", a)] = keep("words_h%d" % a, [P, T], U32)
            plane[("h", a)] = keep("plane_h%d" % a, [P, T], U8)
        result = [keep("result%d" % t, [P, M], F32) for t in range(T // P)]
        w_codes = [keep("w_codes%d" % nh, [P, 2, 2 * HALF], U8) for nh in range(2)]
        w_plane = keep("w_plane", [P, 2, M], U8)
        b_rows = keep("b_rows", [P, M // P], F32)
        bias = keep("bias", [P, M], F32)
        identity = keep("identity", [P, P], F32)
        warm = keep("warm", [P, 2], F32)

        free = [psum.tile([P, HALF], F32, name="bank%d" % i) for i in range(BANKS)]
        held = {}

        def take_bank(key):
            held[key] = free.pop(0)
            return held[key]

        def return_bank(key):
            free.append(held.pop(key))

        def load(half, i=0):
            width = raw[half][i].shape[2]
            first = half[1] * HALF + i * width
            rows = source[half[0]][:, first:first + width].rearrange("(p j) w -> p j w", j=PACK)
            nc.sync.dma_start(out=raw[half][i][:], in_=rows)

        def load_w_scales():
            for quad in range(4):
                rows = w_scales[:, span(quad, 4), :].rearrange("a q n -> q a n")
                nc.sync.dma_start(out=w_plane[32 * quad:32 * quad + 4, :, :].bitcast(I32), in_=rows.bitcast(I32))

        def load_w_codes(nh):
            rows = w_words[:, :, span(nh, 2 * HALF)].rearrange("a p n -> p a n")
            nc.sync.dma_start(out=w_codes[nh][:].bitcast(I32), in_=rows.bitcast(I32))

        def spread_bias(u):
            bank = take_bank("bias")
            for m in range(4):
                column = b_rows[:, span(4 * u + m, 1)].to_broadcast([P, P])
                nc.tensor.transpose(bank[:, span(m, P)], column, identity[:])
            nc.scalar.copy(out=bias[:].rearrange("q (p m) -> q p m", p=P)[:, :, span(u, 4)],
                           in_=bank[:].rearrange("q (m p) -> q p m", p=P))
            return_bank("bias")

        def round_weight(copy, half, pair, i=0):
            count = raw[half][i].shape[2] // PACK
            dst = rounded[half][:].rearrange("p (s m j) -> p m j s", s=PACK, j=PACK)
            src = raw[half][i][:].rearrange("p j (m s) -> p m j s", s=PACK)
            copy(out=dst[:, span(i, count), :, span(pair, 2)], in_=src[:, :, :, span(pair, 2)])

        def round_last_x():
            nc.gpsimd.tensor_scalar(out=rounded[("x", 1)][:, span(0, PACK * QUARTER)].rearrange("p (w j) -> p w j", j=PACK),
                                    in0=raw[("x", 1)][1][:].rearrange("p j w -> p w j"),
                                    scalar1=1.0, scalar2=0.0, op0=ALU.mult, op1=ALU.add)

        def round_stream(copy, half, first, count):
            i, start = divmod(first * P, raw[half][0].shape[2])
            dst = rounded[half][:, span(first, PACK * P, count)].rearrange("p (u v j) -> p u j v", v=RUN, j=PACK)
            src = raw[half][i][:, :, start:start + count * P].rearrange("p j (u v) -> p u j v", v=RUN)
            copy(out=dst, in_=src)

        def quantise(half, first, count, read_from=None):
            cols = span(first, P, count)
            values = rounded[half][:, span(first if read_from is None else read_from, PACK * P, count)]
            nc.vector.quantize_mx(out=words[half][:, cols].bitcast(E5M2 if half[0] == "c" else E4M3),
                                  scales=plane[half][:, cols], in_=values)

        def project_c(a, th, j):
            nc.tensor.matmul_mx(out=take_bank(("pc", a, th, j))[:],
                                lhsT=words[("wc", a)][:, span(j, P)].bitcast(E4M3), lhsT_scale=plane[("wc", a)][:, span(j, P)],
                                rhs=words[("c", th)][:].bitcast(E5M2), rhs_scale=plane[("c", th)][:], start=True, stop=True)

        def drain_c(a, th, j, copy=on_scalar):
            copy(out=pc[(a, th)][:, j, :], in_=held[("pc", a, th, j)][:])
            return_bank(("pc", a, th, j))

        def project_x(a, t):
            bank = take_bank(("px", a, t))
            th, cols = t // 4, span(t % 4, P)
            for j in range(PACK):
                nc.tensor.matmul_mx(out=bank[:, span(j, P)],
                                    lhsT=words[("wx", a)][:, span(j, P)].bitcast(E4M3), lhsT_scale=plane[("wx", a)][:, span(j, P)],
                                    rhs=words[("x", th)][:, cols].bitcast(E4M3), rhs_scale=plane[("x", th)][:, cols],
                                    start=True, stop=True)

        def multiply(a, t):
            nc.vector.tensor_tensor(
                out=rounded[("h", a)][:, span(t, PACK * P)].rearrange("p (u v j) -> p u j v", v=RUN, j=PACK),
                in0=held[("px", a, t)][:].rearrange("p (j u v) -> p u j v", j=PACK, v=RUN),
                in1=pc[(a, t // 4)][:, :, span(t % 4, P)].rearrange("p j (u v) -> p u j v", v=RUN),
                op=ALU.mult)
            return_bank(("px", a, t))

        def project_out(t, nh):
            bank = take_bank(("y", t, nh))
            for a in range(2):
                nc.tensor.matmul_mx(out=bank[:],
                                    lhsT=words[("h", a)][:, span(t, P)].bitcast(E4M3), lhsT_scale=plane[("h", a)][:, span(t, P)],
                                    rhs=w_codes[nh][:, a, :].bitcast(E2M1), rhs_scale=w_plane[:, a, span(nh, HALF)],
                                    start=(a == 0), stop=(a == 1))

        def add_bias(t, nh, first=0, width=HALF):
            cols = slice(nh * HALF + first, nh * HALF + first + width)
            nc.vector.tensor_tensor(out=result[t][:, cols], in0=held[("y", t, nh)][:, first:first + width],
                                    in1=bias[:, cols], op=ALU.add)
            if first + width == HALF:
                return_bank(("y", t, nh))

        def drain_out(t, nh):
            nc.scalar.copy(out=result[t][:, span(nh, HALF)], in_=held[("y", t, nh)][:])
            return_bank(("y", t, nh))

        def add_bias_gpsimd(t, nh, spare):
            nc.gpsimd.tensor_tensor(out=spare, in0=result[t][:, span(nh, HALF)], in1=bias[:, span(nh, HALF)], op=ALU.add)

        def gelu(t, first, width, values=None):
            cols = slice(first, first + width)
            nc.scalar.activation(out=result[t][:, cols], in_=result[t][:, cols] if values is None else values, func=GELU)

        def store(t, first, width):
            cols = slice(first, first + width)
            nc.sync.dma_start(out=out[span(t, P), cols], in_=result[t][:, cols])

        def finish(t, first, width):
            gelu(t, first, width)
            store(t, first, width)

        ctx.enter_context(tc.manual_schedule())

        nc.scalar.dma_start(out=b_rows[:], in_=b.rearrange("(p m) -> p m", p=P))
        nc.vector.memset(warm[:, 0:1], 0.0)
        make_identity(nc, identity[:])
        nc.vector.memset(w_plane[:].rearrange("p a n -> p (a n)").bitcast(U32), 0)

        for half in (("wc", 0), ("c", 0), ("wx", 0), ("x", 0), ("wc", 1), ("wx", 1), ("c", 1)):
            for i in range(PIECES[half]):
                load(half, i)
        load_w_scales()
        for nh in range(2):
            load_w_codes(nh)
        for i in range(2):
            load(("x", 1), i)

        nc.scalar.activation(out=warm[:, 1:2], in_=warm[:, 0:1], func=GELU)

        round_weight(on_vector, ("wc", 0), 0)
        round_weight(on_scalar, ("wc", 0), 1)
        quantise(("wc", 0), 0, 2)
        for u in range(2):
            spread_bias(u)
        round_stream(on_vector, ("c", 0), 0, 2)
        quantise(("wc", 0), 2, 2)
        round_stream(on_scalar, ("c", 0), 2, 2)
        quantise(("c", 0), 0, 4)
        for j in range(PACK):
            project_c(0, 0, j)
        round_weight(on_vector, ("wx", 0), 0)
        round_weight(on_scalar, ("wx", 0), 1)
        quantise(("wx", 0), 0, 2)
        round_stream(on_vector, ("x", 0), 0, 2)
        quantise(("wx", 0), 2, 2)
        quantise(("x", 0), 0, 2)
        round_stream(on_vector, ("x", 0), 2, 2)
        quantise(("x", 0), 2, 2)
        for j in range(PACK):
            drain_c(0, 0, j)
        for t in range(4):
            project_x(0, t)
        for t in range(4):
            multiply(0, t)

        for i in range(2):
            for pair in range(2):
                round_weight(on_scalar, ("wc", 1), pair, i)
        for pair in range(2):
            quantise(("wc", 1), 2 * pair, 2)
        quantise(("h", 0), 0, 4)
        for j in range(PACK):
            project_c(1, 0, j)
        for i, copy in enumerate((on_scalar, on_vector)):
            for pair in range(2):
                round_weight(copy, ("wx", 1), pair, i)
        for pair in range(2):
            quantise(("wx", 1), 2 * pair, 2)
        for j in range(PACK):
            drain_c(1, 0, j, on_vector if j == PACK - 1 else on_scalar)

        for t in range(4):
            project_x(1, t)
        for first in (0, 2):
            round_stream(on_scalar, ("c", 1), first, 2)
        multiply(1, 0)
        multiply(1, 1)
        quantise(("h", 1), 0, 1)
        multiply(1, 2)
        quantise(("h", 1), 1, 1)
        for t in range(2):
            for nh in range(2):
                project_out(t, nh)
        multiply(1, 3)
        drain_out(0, 0)
        quantise(("c", 1), 0, 4)
        quantise(("h", 1), 2, 2)
        spare0 = rounded[("h", 1)][:, span(2, PACK * P, 2)].bitcast(F32)
        add_bias_gpsimd(0, 0, spare0)
        project_c(0, 1, 0)
        project_c(0, 1, 1)
        round_stream(on_scalar, ("x", 1), 0, 2)
        add_bias(0, 1)
        project_c(0, 1, 2)
        add_bias(1, 0)
        project_c(0, 1, 3)
        drain_c(0, 1, 0)
        project_out(2, 0)
        add_bias(1, 1)
        drain_c(0, 1, 1)
        project_c(1, 1, 0)
        quantise(("x", 1), 0, 2)
        round_last_x()
        project_out(2, 1)
        drain_c(0, 1, 2)
        project_out(3, 0)
        drain_c(0, 1, 3)
        add_bias(2, 0)
        project_c(1, 1, 1)
        project_out(3, 1)
        add_bias(2, 1)
        drain_c(1, 1, 0)
        drain_c(1, 1, 1)
        project_x(0, 4)
        add_bias(3, 0)
        project_x(0, 5)
        drain_out(3, 1)
        quantise(("x", 1), 2, 2, read_from=0)
        spare3 = rounded[("x", 1)][:, span(0, PACK * QUARTER)].bitcast(F32)
        add_bias_gpsimd(3, 1, spare3)
        project_c(1, 1, 2)
        project_c(1, 1, 3)
        project_x(0, 6)
        multiply(0, 4)
        project_x(0, 7)
        drain_c(1, 1, 2)
        multiply(0, 5)
        drain_c(1, 1, 3)

        project_x(1, 4)
        project_x(1, 5)
        multiply(0, 6)
        multiply(0, 7)
        project_x(1, 6)
        project_x(1, 7)
        gelu(0, 0, HALF, spare0)
        gelu(0, HALF, HALF)
        store(0, 0, M)
        for t in (1, 2):
            finish(t, 0, M)
        gelu(3, 0, HALF)
        gelu(3, HALF, HALF, spare3)
        store(3, 0, M)
        multiply(1, 4)
        quantise(("h", 0), 4, 4)
        quantise(("h", 1), 4, 1)
        project_out(4, 0)
        project_out(4, 1)
        multiply(1, 5)
        for t in (5, 6):
            multiply(1, t + 1)
            quantise(("h", 1), t, 1)
            project_out(t, 0)
            project_out(t, 1)
        add_bias(4, 0)
        add_bias(4, 1)
        quantise(("h", 1), 7, 1)
        project_out(7, 0)
        project_out(7, 1)
        add_bias(5, 0)

        finish(4, 0, HALF)
        finish(4, HALF, HALF)
        add_bias(5, 1)
        finish(5, 0, HALF)
        finish(5, HALF, HALF)
        for nh in range(2):
            add_bias(6, nh)
            finish(6, nh * HALF, HALF)
        add_bias(7, 0)
        finish(7, 0, HALF)
        for first in (0, QUARTER):
            add_bias(7, 1, first, QUARTER)
            finish(7, HALF + first, QUARTER)
